import numpy as np
import ml_dtypes


def mxq(x, axis, fmt="e4m3"):
    dtype, down = {"e4m3": (ml_dtypes.float8_e4m3fn, 7), "e5m2": (ml_dtypes.float8_e5m2, 14)}[fmt]
    v = np.moveaxis(np.asarray(x, np.float32).astype(ml_dtypes.bfloat16).astype(np.float64), axis, -1)
    blocks = v.reshape(v.shape[:-1] + (-1, 32))
    amax = np.abs(blocks).max(-1, keepdims=True)
    byte = np.maximum(np.where(amax > 0, np.frexp(amax)[1] - 1 + 127, 0) - down, 1)
    scale = np.exp2(byte - 127.0)
    codes = (blocks / scale).astype(np.float32).astype(dtype).astype(np.float64)
    return np.moveaxis((codes * scale).reshape(v.shape), -1, axis)


WIDE = False


def mx_kscale(k):
    if not WIDE:
        return np.ones(k)
    levels = np.array([10, -10, 5, -5, 0])
    if k % 512:
        return np.exp2(np.random.permutation(np.resize(levels, k // 32))).repeat(32)
    a = np.empty((k // 512, 16))
    for p in range(k // 512):
        a[p, :8] = np.random.permutation(np.resize(levels, 8))
        for g in range(8):
            far = levels[np.abs(levels - a[p, g]) >= 10]
            a[p, g + 8] = far[np.random.randint(len(far))]
    return np.exp2(a.ravel()).repeat(32)


def f64(x):
    return np.asarray(x).astype(np.float64)


def striped(idx):
    return np.tile(np.asarray(idx).reshape(-1, 16).T, (8, 1)).astype(np.uint16)


def unstriped(offs):
    return offs[:16].T.reshape(-1).astype(np.int64)


E2M1 = np.array([0.0, 0.5, 1.0, 1.5, 2.0, 3.0, 4.0, 6.0, -0.0, -0.5, -1.0, -1.5, -2.0, -3.0, -4.0, -6.0])


def pack_weight(w, fmt):
    k, n = w.shape
    w = f64(np.asarray(w, np.float32).astype(ml_dtypes.bfloat16)).reshape(k // 32, 32, n)
    amax = np.abs(w).max(1)
    if fmt == "e4m3":
        byte = np.frexp(amax)[1] - 1 + 127 - 7
    else:
        mant, ex = np.frexp(amax / 6.0)
        byte = np.where(mant > 0.5, ex, ex - 1) + 127
    byte = np.clip(np.where(amax > 0, byte, 1), 1, 254)
    scaled = (w * np.exp2(127.0 - byte)[:, None, :]).reshape(k, n).astype(np.float32)
    by_word = np.ascontiguousarray(scaled.reshape(k // 512, 128, 4, n).transpose(0, 1, 3, 2))
    if fmt == "e4m3":
        words = by_word.astype(ml_dtypes.float8_e4m3fn).view(np.uint8)
    else:
        c = by_word.astype(ml_dtypes.float4_e2m1fn).view(np.uint8) & 0xF
        words = (c[..., 0::2] | (c[..., 1::2] << 4)).reshape(k // 512, 128, 2 * n)
    return np.ascontiguousarray(words), np.ascontiguousarray(byte.astype(np.uint8).reshape(k // 512, 16, n))


def unpack_weight(words, scales, fmt):
    g, _, n = scales.shape
    words = np.ascontiguousarray(words).reshape(g, 128, n, -1)
    if fmt == "e4m3":
        vals = words.view(ml_dtypes.float8_e4m3fn).astype(np.float64)
    else:
        nib = np.empty((g, 128, n, 4), np.uint8)
        nib[..., 0::2] = words & 0xF
        nib[..., 1::2] = words >> 4
        vals = E2M1[nib]
    vals = vals * np.repeat(np.exp2(scales.astype(np.float64) - 127.0), 8, axis=1)[..., None]
    return vals.transpose(0, 1, 3, 2).reshape(g * 512, n)


def softplus(v):
    return np.log(1.0 + np.exp(v))


def sigmoid(v):
    return 1.0 / (1.0 + np.exp(-v))


D, E, T, I, Q = 512, 512, 2048, 512, 128


def setup_inputs():
    n = np.random.standard_normal
    idx = np.random.permutation(T)[:I]
    fd = mx_kscale(D)
    fe = mx_kscale(E)
    keysp = pack_weight(n((D, T)) / fd[:, None], "e4m3")
    valsp = pack_weight(n((E, T)) / fe[:, None], "e4m3")
    return {
        "query": (n((D, Q)) * 0.6 / np.sqrt(D) * fd[:, None]).astype(np.float32),
        "query2": (n((D, Q)) * 1.0 / np.sqrt(D) * fd[:, None]).astype(np.float32),
        "keys_words": keysp[0],
        "keys_scales": keysp[1],
        "strict": (np.random.uniform(0.4, 1.2, (Q, 1))).astype(np.float32),
        "gout": (n((E, Q)) * 1 / np.sqrt(E) * fe[:, None]).astype(np.float32),
        "vals_words": valsp[0],
        "vals_scales": valsp[1],
        "base": (0.5 * n((Q, I))).astype(np.float32),
        "offs": striped(idx),
    }


def reference(query, query2, keys_words, keys_scales, strict, gout, vals_words, vals_scales, base, offs):
    idx = unstriped(offs)
    keysu = unpack_weight(keys_words, keys_scales, "e4m3")
    valsu = unpack_weight(vals_words, vals_scales, "e4m3")
    queryq = mxq(f64(query), 0, "e4m3")
    keysidxg = keysu[:, idx]
    a = queryq.T @ keysidxg
    query2q = mxq(f64(query2), 0, "e4m3")
    b = query2q.T @ keysidxg
    s = a - softplus(b) * f64(strict)
    p = np.exp(s - np.max(s, axis=1, keepdims=True))
    z = np.sum(p, axis=1, keepdims=True)
    goutq = mxq(f64(gout), 0, "e4m3")
    valsidxg = valsu[:, idx]
    c0 = goutq.T @ valsidxg
    dz = np.sum(c0 * p / np.square(z) * (-1.0), axis=1, keepdims=True)
    dp = c0 / z + dz
    ds = dp * p
    db = ds * (-1.0) * f64(strict) * sigmoid(b)
    hdb = db * 512.0 * 2.0 * 512.0
    hds = hdb * sigmoid(b) * f64(strict) * (-1.0)
    hdp = hds * p
    hdz = np.sum(hdp, axis=1, keepdims=True)
    hz = np.sum(hdp * c0 / np.square(z) * (-1.0), axis=1, keepdims=True) + np.sum(hdz * (-1.0) * c0 * p / np.square(np.square(z)) * (-1.0), axis=1, keepdims=True) * z * 2.0
    hp = hds * dp + hdz * (-1.0) / np.square(z) * c0 + hz
    hs = hp * p
    hb = hdb * ds * (-1.0) * f64(strict) * sigmoid(b) * (1.0 - sigmoid(b)) + hs * (-1.0) * f64(strict) * sigmoid(b)
    y = hb + f64(base)
    return y

@@ -1,0 +1,187 @@
+import math
+from contextlib import ExitStack
+
+import concourse.mybir as mybir
+
+D, E, T, SLOTS, Q = 512, 512, 2048, 512, 128
+FLOPS = 3 * 2 * Q * SLOTS * D
+
+F32 = mybir.dt.float32
+BF16 = mybir.dt.bfloat16
+I32 = mybir.dt.int32
+U32 = mybir.dt.uint32
+U16 = mybir.dt.uint16
+U8 = mybir.dt.uint8
+FP8X4 = mybir.dt.float8_e4m3fn_x4
+ALU = mybir.AluOpType
+ACT = mybir.ActivationFunctionType
+AXIS_X = mybir.AxisListType.X
+
+P = 128
+PACK = 4
+HALF = SLOTS // 2
+LIST_ROWS = 16
+CAP = 40.0
+ROOT_K = 512.0 * math.sqrt(2.0)
+
+
+def tile_attend_gpheldback_kernel(tc, query, query2, keys_words, keys_scales, strict, gout, vals_words, vals_scales, base, offs, out):
+    nc = tc.nc
+    halves = [slice(h * HALF, (h + 1) * HALF) for h in range(2)]
+
+    with ExitStack() as ctx:
+        held = ctx.enter_context(tc.tile_pool(name="held", bufs=1))
+        psum = ctx.enter_context(tc.psum_pool(name="psum", bufs=1))
+
+        def wide(name, tag=None):
+            return held.tile([P, SLOTS], F32, name=name, tag=tag or name)
+
+        def column(name, n=1):
+            return held.tile([P, n], F32, name=name)
+
+        def load_rows(queue, name, rows):
+            raw = held.tile([P, PACK, Q], F32, name=name)
+            queue.dma_start(out=raw[:], in_=rows.rearrange("(p j) c -> p j c", j=PACK))
+            return raw
+
+        def load_words(name, words):
+            pool_words = held.tile([P, T], U32, name=name)
+            nc.sync.dma_start(out=pool_words[:].bitcast(I32), in_=words[0].rearrange("p n j -> p (n j)").bitcast(I32))
+            return pool_words
+
+        def load_scales(plane, scales):
+            for r in range(4):
+                nc.sync.dma_start(out=plane[r:P:32, :].bitcast(I32), in_=scales[0][r:16:4, :].bitcast(I32))
+
+        def quantise(name, grouped):
+            codes = held.tile([P, Q], U32, name=name + "_codes", align_bytes=64)
+            plane = held.tile([P, Q], U8, name=name + "_plane", align_bytes=64)
+            nc.vector.quantize_mx(out=codes[:].bitcast(FP8X4), scales=plane[:], in_=grouped[:].rearrange("p c j -> p (c j)"))
+            return codes, plane
+
+        def product(acc, rows, words, plane):
+            nc.tensor.matmul_mx(out=acc, lhsT=rows[0][:].bitcast(FP8X4), lhsT_scale=rows[1][:], rhs=words.bitcast(FP8X4), rhs_scale=plane, start=True, stop=True)
+
+        key_plane = held.tile([P, T], U8, name="key_plane")
+        val_plane = held.tile([P, T], U8, name="val_plane")
+        nc.gpsimd.memset(key_plane[:].bitcast(I32), 0)
+        nc.vector.memset(val_plane[:].bitcast(I32), 0)
+        val_plane_mx = held.tile([P, SLOTS], U8, name="val_plane_mx", align_bytes=64)
+        nc.gpsimd.memset(val_plane_mx[:].bitcast(I32), 0)
+
+        offsets = held.tile([P, SLOTS // LIST_ROWS], U16, name="offsets")
+        nc.sync.dma_start(offsets[:], offs)
+        query2_raw = load_rows(nc.scalar, "query2_raw", query2)
+        load_scales(key_plane, keys_scales)
+        nc.sync.dma_start(out=val_plane[0:P:8, :].bitcast(I32), in_=vals_scales[0].bitcast(I32))
+        key_words = load_words("key_words", keys_words)
+        query_raw = load_rows(nc.sync, "query_raw", query)
+        strictness = column("strictness")
+        nc.sync.dma_start(out=strictness[:], in_=strict)
+        val_words = load_words("val_words", vals_words)
+        gout_raw = load_rows(nc.sync, "gout_raw", gout)
+
+        query2_bf = held.tile([P, Q, PACK], BF16, name="query2_bf", align_bytes=64)
+        nc.scalar.activation(out=query2_bf[:], in_=query2_raw[:].rearrange("p j c -> p c j"), func=ACT.Copy)
+
+        key_plane_g = held.tile([P, SLOTS], U8, name="key_plane_g", align_bytes=64)
+        nc.vector.tensor_copy(key_plane_g[:], key_plane[:].indirect(offsets[:]))
+        val_plane_g = held.tile([P, SLOTS], U8, name="val_plane_g", align_bytes=64)
+        nc.vector.tensor_copy(val_plane_g[:], val_plane[:].indirect(offsets[:]))
+        for r in range(4):
+            nc.sync.dma_start(out=val_plane_mx[r:P:32, :].bitcast(I32), in_=val_plane_g[8 * r : P : 32, :].bitcast(I32))
+        base_sb = wide("base_sb")
+        nc.sync.dma_start(out=base_sb[:], in_=base)
+        query2_mx = quantise("query2", query2_bf)
+        key_words_g = held.tile([P, SLOTS], U32, name="key_words_g", align_bytes=64)
+        b_half = [psum.tile([P, HALF], F32, name="b_half%d" % h) for h in range(2)]
+        exp_b = wide("exp_b", tag="query_raw")
+        cols = HALF // LIST_ROWS
+        for h in range(2):
+            nc.vector.tensor_copy(key_words_g[:, halves[h]], key_words[:].indirect(offsets[:, h * cols : (h + 1) * cols]))
+            product(b_half[h][:], query2_mx, key_words_g[:, halves[h]], key_plane_g[:, halves[h]])
+
+        query_bf = held.tile([P, Q, PACK], BF16, name="query_bf", align_bytes=64)
+        nc.scalar.activation(out=query_bf[:], in_=query_raw[:].rearrange("p j c -> p c j"), func=ACT.Copy)
+        for h in range(2):
+            nc.scalar.activation(out=exp_b[:, halves[h]], in_=b_half[h][:], func=ACT.Exp)
+        query_mx = quantise("query", query_bf)
+        a_acc = psum.tile([P, SLOTS], F32, name="a_acc")
+        product(a_acc[:], query_mx, key_words_g[:], key_plane_g[:])
+
+        slope = column("slope")
+        strict_pair = column("strict_pair", 2)
+        nc.gpsimd.tensor_scalar(slope[:], strictness[:], -1.0, -1.0, ALU.mult, ALU.add)
+        nc.gpsimd.tensor_scalar(strict_pair[:, 0:1], strictness[:], 1.0, 0.0, ALU.mult, ALU.add)
+        nc.gpsimd.tensor_scalar(strict_pair[:, 1:2], strictness[:], ROOT_K, 0.0, ALU.mult, ALU.add)
+
+        exp_capped = wide("exp_capped")
+        log_part = wide("log_part")
+        for h in range(2):
+            nc.gpsimd.tensor_scalar(exp_capped[:, halves[h]], exp_b[:, halves[h]], math.exp(CAP), 0.0, ALU.min, ALU.max)
+        for h in range(2):
+            nc.scalar.activation(out=log_part[:, halves[h]], in_=exp_capped[:, halves[h]], func=ACT.Ln, bias=1.0)
+
+        val_words_g = held.tile([P, SLOTS], U32, name="val_words_g", align_bytes=64)
+        nc.vector.tensor_copy(val_words_g[:], val_words[:].indirect(offsets[:]))
+
+        gout_bf = held.tile([P, Q, PACK], BF16, name="gout_bf", align_bytes=64)
+        nc.gpsimd.tensor_scalar(gout_bf[:], gout_raw[:].rearrange("p j c -> p c j"), 1.0, 0.0, ALU.mult, ALU.add)
+
+        gout_mx = quantise("gout", gout_bf)
+        c_acc = psum.tile([P, SLOTS], F32, name="c_acc")
+        product(c_acc[:], gout_mx, val_words_g[:], val_plane_mx[:])
+
+        soft = held.tile([P, SLOTS], F32, name="soft", tag="gout_bf", align_bytes=64)
+        for h in range(2):
+            nc.vector.tensor_tensor(soft[:, halves[h]], b_half[h][:], log_part[:, halves[h]], ALU.max)
+        neg_s = wide("neg_s")
+        nc.vector.scalar_tensor_tensor(neg_s[:], soft[:], strictness[:], a_acc[:], ALU.mult, ALU.subtract)
+        neg_max = column("neg_max")
+        nc.vector.tensor_reduce(neg_max[:], neg_s[:], AXIS_X, ALU.min)
+        p = wide("p")
+        z = column("z")
+        nc.scalar.activation(out=p[:], in_=neg_s[:], func=ACT.Exp, bias=neg_max[:], scale=-1.0, accum_out=z[:])
+        log_sig = wide("log_sig")
+        for h in range(2):
+            nc.vector.tensor_tensor(log_sig[:, halves[h]], b_half[h][:], soft[:, halves[h]], ALU.subtract)
+        sig = wide("sig")
+        nc.scalar.activation(out=sig[:], in_=log_sig[:], func=ACT.Exp)
+        neg_s2 = wide("neg_s2")
+        nc.vector.tensor_tensor(neg_s2[:], neg_s[:], log_sig[:], ALU.subtract)
+        t = wide("t")
+        nc.scalar.activation(out=t[:], in_=neg_s2[:], func=ACT.Exp, bias=neg_max[:], scale=-1.0)
+        curve = wide("curve")
+        nc.scalar.activation(out=curve[:], in_=sig[:], func=ACT.Identity, bias=1.0, scale=slope[:])
+        inv_z = column("inv_z")
+        nc.vector.reciprocal(inv_z[:], z[:])
+        c_mean = column("c_mean")
+        weighted = wide("weighted")
+        nc.vector.scalar_tensor_tensor(weighted[:], c_acc[:], inv_z[:], p[:], ALU.mult, ALU.mult, accum_out=c_mean[:])
+        kappa = column("kappa", 2)
+        nc.vector.tensor_scalar(kappa[:], strict_pair[:], inv_z[:], None, ALU.mult)
+        v = wide("v")
+        nc.vector.scalar_tensor_tensor(v[:], c_acc[:], c_mean[:], t[:], ALU.subtract, ALU.mult)
+        cubed = column("cubed")
+        nc.vector.tensor_scalar(cubed[:], kappa[:, 1:2], kappa[:, 1:2], kappa[:, 0:1], ALU.mult, ALU.mult)
+
+        squares = wide("squares")
+        m_sum = column("m_sum")
+        nc.scalar.activation(out=squares[:], in_=v[:], func=ACT.Square, scale=kappa[:, 1:2], accum_out=m_sum[:])
+        m_coef = column("m_coef")
+        nc.scalar.activation(out=m_coef[:], in_=m_sum[:], func=ACT.Copy, scale=kappa[:, 0:1])
+
+        h_terms = wide("h_terms")
+        h_coef = column("h_coef")
+        nc.vector.scalar_tensor_tensor(h_terms[:], v[:], cubed[:], t[:], ALU.mult, ALU.mult, accum_out=h_coef[:])
+        direct = wide("direct")
+        nc.vector.tensor_tensor(direct[:], squares[:], curve[:], ALU.mult)
+        with_h = wide("with_h")
+        nc.vector.scalar_tensor_tensor(with_h[:], v[:], h_coef[:], base_sb[:], ALU.mult, ALU.add)
+        with_m = wide("with_m")
+        for h in range(2):
+            nc.vector.scalar_tensor_tensor(with_m[:, halves[h]], t[:, halves[h]], m_coef[:], direct[:, halves[h]], ALU.mult, ALU.add)
+        result = wide("result")
+        for h in range(2):
+            nc.vector.tensor_tensor(result[:, halves[h]], with_m[:, halves[h]], with_h[:, halves[h]], ALU.add)
+            nc.sync.dma_start(out=out[:, halves[h]], in_=result[:, halves[h]])

@@ -22,6 +22,7 @@ PACK = 4
 HALF = SLOTS // 2
 LIST_ROWS = 16
 CAP = 40.0
+FIRST_STORE = 320
 ROOT_K = 512.0 * math.sqrt(2.0)
 
 
@@ -53,8 +54,8 @@ def tile_attend_gpheldback_kernel(tc, query, query2, keys_words, keys_scales, st
             for r in range(4):
                 nc.sync.dma_start(out=plane[r:P:32, :].bitcast(I32), in_=scales[0][r:16:4, :].bitcast(I32))
 
-        def quantise(name, grouped):
-            codes = held.tile([P, Q], U32, name=name + "_codes", align_bytes=64)
+        def quantise(name, grouped, tag=None):
+            codes = held.tile([P, Q], U32, name=name + "_codes", tag=tag or name + "_codes", align_bytes=64)
             plane = held.tile([P, Q], U8, name=name + "_plane", align_bytes=64)
             nc.vector.quantize_mx(out=codes[:].bitcast(FP8X4), scales=plane[:], in_=grouped[:].rearrange("p c j -> p (c j)"))
             return codes, plane
@@ -64,32 +65,33 @@ def tile_attend_gpheldback_kernel(tc, query, query2, keys_words, keys_scales, st
 
         key_plane = held.tile([P, T], U8, name="key_plane")
         val_plane = held.tile([P, T], U8, name="val_plane")
-        nc.gpsimd.memset(key_plane[:].bitcast(I32), 0)
-        nc.vector.memset(val_plane[:].bitcast(I32), 0)
+        nc.vector.memset(key_plane[:, : T // 2].bitcast(I32), 0)
+        nc.gpsimd.memset(key_plane[:, T // 2 :].bitcast(I32), 0)
+        nc.vector.memset(val_plane[: P - 16, :].bitcast(I32), 0)
         val_plane_mx = held.tile([P, SLOTS], U8, name="val_plane_mx", align_bytes=64)
         nc.gpsimd.memset(val_plane_mx[:].bitcast(I32), 0)
 
+        query2_raw = load_rows(nc.sync, "query2_raw", query2)
         offsets = held.tile([P, SLOTS // LIST_ROWS], U16, name="offsets")
         nc.sync.dma_start(offsets[:], offs)
-        query2_raw = load_rows(nc.scalar, "query2_raw", query2)
+        nc.sync.dma_start(out=val_plane[P - 16 :, :].bitcast(I32), in_=vals_scales[0].bitcast(I32))
         load_scales(key_plane, keys_scales)
-        nc.sync.dma_start(out=val_plane[0:P:8, :].bitcast(I32), in_=vals_scales[0].bitcast(I32))
         key_words = load_words("key_words", keys_words)
         query_raw = load_rows(nc.sync, "query_raw", query)
-        strictness = column("strictness")
-        nc.sync.dma_start(out=strictness[:], in_=strict)
         val_words = load_words("val_words", vals_words)
         gout_raw = load_rows(nc.sync, "gout_raw", gout)
+        strictness = column("strictness")
+        nc.sync.dma_start(out=strictness[:], in_=strict)
 
         query2_bf = held.tile([P, Q, PACK], BF16, name="query2_bf", align_bytes=64)
         nc.scalar.activation(out=query2_bf[:], in_=query2_raw[:].rearrange("p j c -> p c j"), func=ACT.Copy)
 
-        key_plane_g = held.tile([P, SLOTS], U8, name="key_plane_g", align_bytes=64)
-        nc.vector.tensor_copy(key_plane_g[:], key_plane[:].indirect(offsets[:]))
         val_plane_g = held.tile([P, SLOTS], U8, name="val_plane_g", align_bytes=64)
         nc.vector.tensor_copy(val_plane_g[:], val_plane[:].indirect(offsets[:]))
+        key_plane_g = held.tile([P, SLOTS], U8, name="key_plane_g", align_bytes=64)
+        nc.vector.tensor_copy(key_plane_g[:], key_plane[:].indirect(offsets[:]))
         for r in range(4):
-            nc.sync.dma_start(out=val_plane_mx[r:P:32, :].bitcast(I32), in_=val_plane_g[8 * r : P : 32, :].bitcast(I32))
+            nc.sync.dma_start(out=val_plane_mx[r:P:32, :].bitcast(I32), in_=val_plane_g[P - 16 + r : P : 4, :].bitcast(I32))
         base_sb = wide("base_sb")
         nc.sync.dma_start(out=base_sb[:], in_=base)
         query2_mx = quantise("query2", query2_bf)
@@ -109,16 +111,10 @@ def tile_attend_gpheldback_kernel(tc, query, query2, keys_words, keys_scales, st
         a_acc = psum.tile([P, SLOTS], F32, name="a_acc")
         product(a_acc[:], query_mx, key_words_g[:], key_plane_g[:])
 
-        slope = column("slope")
-        strict_pair = column("strict_pair", 2)
-        nc.gpsimd.tensor_scalar(slope[:], strictness[:], -1.0, -1.0, ALU.mult, ALU.add)
-        nc.gpsimd.tensor_scalar(strict_pair[:, 0:1], strictness[:], 1.0, 0.0, ALU.mult, ALU.add)
-        nc.gpsimd.tensor_scalar(strict_pair[:, 1:2], strictness[:], ROOT_K, 0.0, ALU.mult, ALU.add)
-
         exp_capped = wide("exp_capped")
-        log_part = wide("log_part")
+        log_part = held.tile([P, SLOTS], F32, name="log_part", align_bytes=64)
         for h in range(2):
-            nc.gpsimd.tensor_scalar(exp_capped[:, halves[h]], exp_b[:, halves[h]], math.exp(CAP), 0.0, ALU.min, ALU.max)
+            nc.vector.tensor_scalar(exp_capped[:, halves[h]], exp_b[:, halves[h]], math.exp(CAP), 0.0, ALU.min, ALU.max)
         for h in range(2):
             nc.scalar.activation(out=log_part[:, halves[h]], in_=exp_capped[:, halves[h]], func=ACT.Ln, bias=1.0)
 
@@ -128,15 +124,21 @@ def tile_attend_gpheldback_kernel(tc, query, query2, keys_words, keys_scales, st
         gout_bf = held.tile([P, Q, PACK], BF16, name="gout_bf", align_bytes=64)
         nc.gpsimd.tensor_scalar(gout_bf[:], gout_raw[:].rearrange("p j c -> p c j"), 1.0, 0.0, ALU.mult, ALU.add)
 
-        gout_mx = quantise("gout", gout_bf)
-        c_acc = psum.tile([P, SLOTS], F32, name="c_acc")
-        product(c_acc[:], gout_mx, val_words_g[:], val_plane_mx[:])
+        slope = column("slope")
+        strict_pair = column("strict_pair", 2)
+        nc.gpsimd.tensor_scalar(slope[:], strictness[:], -1.0, -1.0, ALU.mult, ALU.add)
+        nc.gpsimd.tensor_scalar(strict_pair[:, 0:1], strictness[:], 1.0, 0.0, ALU.mult, ALU.add)
+        nc.gpsimd.tensor_scalar(strict_pair[:, 1:2], strictness[:], ROOT_K, 0.0, ALU.mult, ALU.add)
 
-        soft = held.tile([P, SLOTS], F32, name="soft", tag="gout_bf", align_bytes=64)
+        soft = wide("soft", tag="val_words")
         for h in range(2):
             nc.vector.tensor_tensor(soft[:, halves[h]], b_half[h][:], log_part[:, halves[h]], ALU.max)
         neg_s = wide("neg_s")
-        nc.vector.scalar_tensor_tensor(neg_s[:], soft[:], strictness[:], a_acc[:], ALU.mult, ALU.subtract)
+        for h in range(2):
+            nc.vector.scalar_tensor_tensor(neg_s[:, halves[h]], soft[:, halves[h]], strictness[:], a_acc[:, halves[h]], ALU.mult, ALU.subtract)
+        gout_mx = quantise("gout", gout_bf, tag="log_part")
+        c_acc = psum.tile([P, SLOTS], F32, name="c_acc")
+        product(c_acc[:], gout_mx, val_words_g[:], val_plane_mx[:])
         neg_max = column("neg_max")
         nc.vector.tensor_reduce(neg_max[:], neg_s[:], AXIS_X, ALU.min)
         p = wide("p")
@@ -147,8 +149,9 @@ def tile_attend_gpheldback_kernel(tc, query, query2, keys_words, keys_scales, st
             nc.vector.tensor_tensor(log_sig[:, halves[h]], b_half[h][:], soft[:, halves[h]], ALU.subtract)
         sig = wide("sig")
         nc.scalar.activation(out=sig[:], in_=log_sig[:], func=ACT.Exp)
-        neg_s2 = wide("neg_s2")
-        nc.vector.tensor_tensor(neg_s2[:], neg_s[:], log_sig[:], ALU.subtract)
+        neg_s2 = held.tile([P, SLOTS], F32, name="neg_s2", tag="gout_bf", align_bytes=64)
+        for h in range(2):
+            nc.vector.tensor_tensor(neg_s2[:, halves[h]], neg_s[:, halves[h]], log_sig[:, halves[h]], ALU.subtract)
         t = wide("t")
         nc.scalar.activation(out=t[:], in_=neg_s2[:], func=ACT.Exp, bias=neg_max[:], scale=-1.0)
         curve = wide("curve")
@@ -179,9 +182,10 @@ def tile_attend_gpheldback_kernel(tc, query, query2, keys_words, keys_scales, st
         with_h = wide("with_h")
         nc.vector.scalar_tensor_tensor(with_h[:], v[:], h_coef[:], base_sb[:], ALU.mult, ALU.add)
         with_m = wide("with_m")
-        for h in range(2):
-            nc.vector.scalar_tensor_tensor(with_m[:, halves[h]], t[:, halves[h]], m_coef[:], direct[:, halves[h]], ALU.mult, ALU.add)
+        parts = [slice(0, FIRST_STORE), slice(FIRST_STORE, SLOTS)]
+        for part in parts:
+            nc.vector.scalar_tensor_tensor(with_m[:, part], t[:, part], m_coef[:], direct[:, part], ALU.mult, ALU.add)
         result = wide("result")
-        for h in range(2):
-            nc.vector.tensor_tensor(result[:, halves[h]], with_m[:, halves[h]], with_h[:, halves[h]], ALU.add)
-            nc.sync.dma_start(out=out[:, halves[h]], in_=result[:, halves[h]])
+        for part in parts:
+            nc.vector.tensor_tensor(result[:, part], with_m[:, part], with_h[:, part], ALU.add)
+            nc.sync.dma_start(out=out[:, part], in_=result[:, part])

@@ -22,7 +22,7 @@ PACK = 4
 HALF = SLOTS // 2
 LIST_ROWS = 16
 CAP = 40.0
-FIRST_STORE = 320
+FIRST_STORE = 256
 ROOT_K = 512.0 * math.sqrt(2.0)
 
 
@@ -37,8 +37,8 @@ def tile_attend_gpheldback_kernel(tc, query, query2, keys_words, keys_scales, st
         def wide(name, tag=None):
             return held.tile([P, SLOTS], F32, name=name, tag=tag or name)
 
-        def column(name, n=1):
-            return held.tile([P, n], F32, name=name)
+        def column(name, n=1, tag=None):
+            return held.tile([P, n], F32, name=name, tag=tag or name)
 
         def load_rows(queue, name, rows):
             raw = held.tile([P, PACK, Q], F32, name=name)
@@ -82,6 +82,8 @@ def tile_attend_gpheldback_kernel(tc, query, query2, keys_words, keys_scales, st
         gout_raw = load_rows(nc.sync, "gout_raw", gout)
         strictness = column("strictness")
         nc.sync.dma_start(out=strictness[:], in_=strict)
+        base_sb = wide("base_sb")
+        nc.sync.dma_start(out=base_sb[:], in_=base)
 
         query2_bf = held.tile([P, Q, PACK], BF16, name="query2_bf", align_bytes=64)
         nc.scalar.activation(out=query2_bf[:], in_=query2_raw[:].rearrange("p j c -> p c j"), func=ACT.Copy)
@@ -92,8 +94,6 @@ def tile_attend_gpheldback_kernel(tc, query, query2, keys_words, keys_scales, st
         nc.vector.tensor_copy(key_plane_g[:], key_plane[:].indirect(offsets[:]))
         for r in range(4):
             nc.sync.dma_start(out=val_plane_mx[r:P:32, :].bitcast(I32), in_=val_plane_g[P - 16 + r : P : 4, :].bitcast(I32))
-        base_sb = wide("base_sb")
-        nc.sync.dma_start(out=base_sb[:], in_=base)
         query2_mx = quantise("query2", query2_bf)
         key_words_g = held.tile([P, SLOTS], U32, name="key_words_g", align_bytes=64)
         b_half = [psum.tile([P, HALF], F32, name="b_half%d" % h) for h in range(2)]
@@ -118,15 +118,22 @@ def tile_attend_gpheldback_kernel(tc, query, query2, keys_words, keys_scales, st
         for h in range(2):
             nc.scalar.activation(out=log_part[:, halves[h]], in_=exp_capped[:, halves[h]], func=ACT.Ln, bias=1.0)
 
+        first, second = halves
+        b_first = column("b_first", HALF)
+        nc.vector.tensor_copy(b_first[:], b_half[0][:])
+        a_plus_b = column("a_plus_b", HALF)
+        nc.vector.tensor_tensor(a_plus_b[:], a_acc[:, first], b_first[:], ALU.add)
         val_words_g = held.tile([P, SLOTS], U32, name="val_words_g", align_bytes=64)
         nc.vector.tensor_copy(val_words_g[:], val_words[:].indirect(offsets[:]))
 
         gout_bf = held.tile([P, Q, PACK], BF16, name="gout_bf", align_bytes=64)
         nc.gpsimd.tensor_scalar(gout_bf[:], gout_raw[:].rearrange("p j c -> p c j"), 1.0, 0.0, ALU.mult, ALU.add)
 
-        slope = column("slope")
+        one_plus = column("one_plus")
+        minus = column("minus")
         strict_pair = column("strict_pair", 2)
-        nc.gpsimd.tensor_scalar(slope[:], strictness[:], -1.0, -1.0, ALU.mult, ALU.add)
+        nc.gpsimd.tensor_scalar(one_plus[:], strictness[:], 1.0, 1.0, ALU.mult, ALU.add)
+        nc.gpsimd.tensor_scalar(minus[:], strictness[:], -1.0, 0.0, ALU.mult, ALU.add)
         nc.gpsimd.tensor_scalar(strict_pair[:, 0:1], strictness[:], 1.0, 0.0, ALU.mult, ALU.add)
         nc.gpsimd.tensor_scalar(strict_pair[:, 1:2], strictness[:], ROOT_K, 0.0, ALU.mult, ALU.add)
 
@@ -144,29 +151,31 @@ def tile_attend_gpheldback_kernel(tc, query, query2, keys_words, keys_scales, st
         p = wide("p")
         z = column("z")
         nc.scalar.activation(out=p[:], in_=neg_s[:], func=ACT.Exp, bias=neg_max[:], scale=-1.0, accum_out=z[:])
-        log_sig = wide("log_sig")
-        for h in range(2):
-            nc.vector.tensor_tensor(log_sig[:, halves[h]], b_half[h][:], soft[:, halves[h]], ALU.subtract)
-        sig = wide("sig")
-        nc.scalar.activation(out=sig[:], in_=log_sig[:], func=ACT.Exp)
+        rest_first = column("rest_first", HALF)
+        nc.scalar.activation(out=rest_first[:], in_=soft[:, first], func=ACT.Exp, scale=-1.0)
         neg_s2 = held.tile([P, SLOTS], F32, name="neg_s2", tag="gout_bf", align_bytes=64)
-        for h in range(2):
-            nc.vector.tensor_tensor(neg_s2[:, halves[h]], neg_s[:, halves[h]], log_sig[:, halves[h]], ALU.subtract)
+        without_b = column("without_b", HALF)
+        nc.vector.scalar_tensor_tensor(without_b[:], soft[:, second], one_plus[:], a_acc[:, second], ALU.mult, ALU.subtract)
+        nc.vector.scalar_tensor_tensor(neg_s2[:, first], soft[:, first], one_plus[:], a_plus_b[:], ALU.mult, ALU.subtract)
+        nc.vector.tensor_tensor(neg_s2[:, second], without_b[:], b_half[1][:], ALU.subtract)
         t = wide("t")
         nc.scalar.activation(out=t[:], in_=neg_s2[:], func=ACT.Exp, bias=neg_max[:], scale=-1.0)
-        curve = wide("curve")
-        nc.scalar.activation(out=curve[:], in_=sig[:], func=ACT.Identity, bias=1.0, scale=slope[:])
+        rest_second = column("rest_second", HALF, tag="neg_s")
+        nc.scalar.activation(out=rest_second[:], in_=soft[:, second], func=ACT.Exp, scale=-1.0)
+        curve = wide("curve", tag="neg_max")
+        for h, rest in enumerate((rest_first, rest_second)):
+            nc.scalar.activation(out=curve[:, halves[h]], in_=rest[:], func=ACT.Identity, bias=minus[:], scale=one_plus[:])
         inv_z = column("inv_z")
         nc.vector.reciprocal(inv_z[:], z[:])
         c_mean = column("c_mean")
         weighted = wide("weighted")
         nc.vector.scalar_tensor_tensor(weighted[:], c_acc[:], inv_z[:], p[:], ALU.mult, ALU.mult, accum_out=c_mean[:])
         kappa = column("kappa", 2)
-        nc.vector.tensor_scalar(kappa[:], strict_pair[:], inv_z[:], None, ALU.mult)
+        nc.gpsimd.tensor_scalar(kappa[:], strict_pair[:], inv_z[:], 0.0, ALU.mult, ALU.add)
         v = wide("v")
         nc.vector.scalar_tensor_tensor(v[:], c_acc[:], c_mean[:], t[:], ALU.subtract, ALU.mult)
         cubed = column("cubed")
-        nc.vector.tensor_scalar(cubed[:], kappa[:, 1:2], kappa[:, 1:2], kappa[:, 0:1], ALU.mult, ALU.mult)
+        nc.gpsimd.tensor_scalar(cubed[:], kappa[:, 1:2], kappa[:, 1:2], kappa[:, 0:1], ALU.mult, ALU.mult)
 
         squares = wide("squares")
         m_sum = column("m_sum")
@@ -179,12 +188,12 @@ def tile_attend_gpheldback_kernel(tc, query, query2, keys_words, keys_scales, st
         nc.vector.scalar_tensor_tensor(h_terms[:], v[:], cubed[:], t[:], ALU.mult, ALU.mult, accum_out=h_coef[:])
         direct = wide("direct")
         nc.vector.tensor_tensor(direct[:], squares[:], curve[:], ALU.mult)
-        with_h = wide("with_h")
-        nc.vector.scalar_tensor_tensor(with_h[:], v[:], h_coef[:], base_sb[:], ALU.mult, ALU.add)
         with_m = wide("with_m")
+        nc.vector.scalar_tensor_tensor(with_m[:], t[:], m_coef[:], base_sb[:], ALU.mult, ALU.add)
+        with_h = wide("with_h")
         parts = [slice(0, FIRST_STORE), slice(FIRST_STORE, SLOTS)]
         for part in parts:
-            nc.vector.scalar_tensor_tensor(with_m[:, part], t[:, part], m_coef[:], direct[:, part], ALU.mult, ALU.add)
+            nc.vector.scalar_tensor_tensor(with_h[:, part], v[:, part], h_coef[:], direct[:, part], ALU.mult, ALU.add)
         result = wide("result")
         for part in parts:
             nc.vector.tensor_tensor(result[:, part], with_m[:, part], with_h[:, part], ALU.add)

@@ -22,7 +22,6 @@ PACK = 4
 HALF = SLOTS // 2
 LIST_ROWS = 16
 CAP = 40.0
-FIRST_STORE = 256
 ROOT_K = 512.0 * math.sqrt(2.0)
 
 
@@ -129,11 +128,11 @@ def tile_attend_gpheldback_kernel(tc, query, query2, keys_words, keys_scales, st
         gout_bf = held.tile([P, Q, PACK], BF16, name="gout_bf", align_bytes=64)
         nc.gpsimd.tensor_scalar(gout_bf[:], gout_raw[:].rearrange("p j c -> p c j"), 1.0, 0.0, ALU.mult, ALU.add)
 
-        one_plus = column("one_plus")
-        minus = column("minus")
+        line = column("line", 2)
+        one_plus = line[:, 0:1]
         strict_pair = column("strict_pair", 2)
-        nc.gpsimd.tensor_scalar(one_plus[:], strictness[:], 1.0, 1.0, ALU.mult, ALU.add)
-        nc.gpsimd.tensor_scalar(minus[:], strictness[:], -1.0, 0.0, ALU.mult, ALU.add)
+        nc.gpsimd.tensor_scalar(one_plus, strictness[:], 1.0, 1.0, ALU.mult, ALU.add)
+        nc.gpsimd.tensor_scalar(line[:, 1:2], strictness[:], -1.0, 0.0, ALU.mult, ALU.add)
         nc.gpsimd.tensor_scalar(strict_pair[:, 0:1], strictness[:], 1.0, 0.0, ALU.mult, ALU.add)
         nc.gpsimd.tensor_scalar(strict_pair[:, 1:2], strictness[:], ROOT_K, 0.0, ALU.mult, ALU.add)
 
@@ -151,20 +150,15 @@ def tile_attend_gpheldback_kernel(tc, query, query2, keys_words, keys_scales, st
         p = wide("p")
         z = column("z")
         nc.scalar.activation(out=p[:], in_=neg_s[:], func=ACT.Exp, bias=neg_max[:], scale=-1.0, accum_out=z[:])
-        rest_first = column("rest_first", HALF)
-        nc.scalar.activation(out=rest_first[:], in_=soft[:, first], func=ACT.Exp, scale=-1.0)
         neg_s2 = held.tile([P, SLOTS], F32, name="neg_s2", tag="gout_bf", align_bytes=64)
         without_b = column("without_b", HALF)
-        nc.vector.scalar_tensor_tensor(without_b[:], soft[:, second], one_plus[:], a_acc[:, second], ALU.mult, ALU.subtract)
-        nc.vector.scalar_tensor_tensor(neg_s2[:, first], soft[:, first], one_plus[:], a_plus_b[:], ALU.mult, ALU.subtract)
+        nc.vector.scalar_tensor_tensor(without_b[:], soft[:, second], one_plus, a_acc[:, second], ALU.mult, ALU.subtract)
+        nc.vector.scalar_tensor_tensor(neg_s2[:, first], soft[:, first], one_plus, a_plus_b[:], ALU.mult, ALU.subtract)
         nc.vector.tensor_tensor(neg_s2[:, second], without_b[:], b_half[1][:], ALU.subtract)
         t = wide("t")
         nc.scalar.activation(out=t[:], in_=neg_s2[:], func=ACT.Exp, bias=neg_max[:], scale=-1.0)
-        rest_second = column("rest_second", HALF, tag="neg_s")
-        nc.scalar.activation(out=rest_second[:], in_=soft[:, second], func=ACT.Exp, scale=-1.0)
-        curve = wide("curve", tag="neg_max")
-        for h, rest in enumerate((rest_first, rest_second)):
-            nc.scalar.activation(out=curve[:, halves[h]], in_=rest[:], func=ACT.Identity, bias=minus[:], scale=one_plus[:])
+        rest = held.tile([P, SLOTS], F32, name="rest", tag="gout_bf", align_bytes=64)
+        nc.scalar.activation(out=rest[:], in_=soft[:], func=ACT.Exp, scale=-1.0)
         inv_z = column("inv_z")
         nc.vector.reciprocal(inv_z[:], z[:])
         c_mean = column("c_mean")
@@ -172,6 +166,10 @@ def tile_attend_gpheldback_kernel(tc, query, query2, keys_words, keys_scales, st
         nc.vector.scalar_tensor_tensor(weighted[:], c_acc[:], inv_z[:], p[:], ALU.mult, ALU.mult, accum_out=c_mean[:])
         kappa = column("kappa", 2)
         nc.gpsimd.tensor_scalar(kappa[:], strict_pair[:], inv_z[:], 0.0, ALU.mult, ALU.add)
+        scaled_line = column("scaled_line", 2)
+        nc.gpsimd.tensor_scalar(scaled_line[:], line[:], kappa[:, 1:2], kappa[:, 1:2], ALU.mult, ALU.mult)
+        curve = wide("curve")
+        nc.scalar.activation(out=curve[:], in_=rest[:], func=ACT.Identity, bias=scaled_line[:, 1:2], scale=scaled_line[:, 0:1])
         v = wide("v")
         nc.vector.scalar_tensor_tensor(v[:], c_acc[:], c_mean[:], t[:], ALU.subtract, ALU.mult)
         cubed = column("cubed")
@@ -186,15 +184,16 @@ def tile_attend_gpheldback_kernel(tc, query, query2, keys_words, keys_scales, st
         h_terms = wide("h_terms")
         h_coef = column("h_coef")
         nc.vector.scalar_tensor_tensor(h_terms[:], v[:], cubed[:], t[:], ALU.mult, ALU.mult, accum_out=h_coef[:])
-        direct = wide("direct")
-        nc.vector.tensor_tensor(direct[:], squares[:], curve[:], ALU.mult)
-        with_m = wide("with_m")
-        nc.vector.scalar_tensor_tensor(with_m[:], t[:], m_coef[:], base_sb[:], ALU.mult, ALU.add)
+        curved = wide("curved")
         with_h = wide("with_h")
-        parts = [slice(0, FIRST_STORE), slice(FIRST_STORE, SLOTS)]
-        for part in parts:
-            nc.vector.scalar_tensor_tensor(with_h[:, part], v[:, part], h_coef[:], direct[:, part], ALU.mult, ALU.add)
+        with_m = wide("with_m")
         result = wide("result")
-        for part in parts:
+        for part in halves:
+            nc.vector.tensor_tensor(curved[:, part], curve[:, part], v[:, part], ALU.mult)
+        for part in halves:
+            nc.vector.scalar_tensor_tensor(with_h[:, part], curved[:, part], h_coef[:], v[:, part], ALU.add, ALU.mult)
+        for part in halves:
+            nc.vector.scalar_tensor_tensor(with_m[:, part], t[:, part], m_coef[:], base_sb[:, part], ALU.mult, ALU.add)
+        for part in halves:
             nc.vector.tensor_tensor(result[:, part], with_m[:, part], with_h[:, part], ALU.add)
             nc.sync.dma_start(out=out[:, part], in_=result[:, part])

import math
from contextlib import ExitStack

import concourse.mybir as mybir

D, E, T, SLOTS, Q = 512, 512, 2048, 512, 128
FLOPS = 3 * 2 * Q * SLOTS * D

F32 = mybir.dt.float32
BF16 = mybir.dt.bfloat16
I32 = mybir.dt.int32
U32 = mybir.dt.uint32
U16 = mybir.dt.uint16
U8 = mybir.dt.uint8
FP8X4 = mybir.dt.float8_e4m3fn_x4
ALU = mybir.AluOpType
ACT = mybir.ActivationFunctionType
AXIS_X = mybir.AxisListType.X

P = 128
PACK = 4
HALF = SLOTS // 2
LIST_ROWS = 16
CAP = 40.0
ROOT_K = 512.0 * math.sqrt(2.0)


def tile_attend_gpheldback_kernel(tc, query, query2, keys_words, keys_scales, strict, gout, vals_words, vals_scales, base, offs, out):
    nc = tc.nc
    halves = [slice(h * HALF, (h + 1) * HALF) for h in range(2)]

    with ExitStack() as ctx:
        held = ctx.enter_context(tc.tile_pool(name="held", bufs=1))
        psum = ctx.enter_context(tc.psum_pool(name="psum", bufs=1))

        def wide(name, tag=None):
            return held.tile([P, SLOTS], F32, name=name, tag=tag or name)

        def column(name, n=1, tag=None):
            return held.tile([P, n], F32, name=name, tag=tag or name)

        def load_rows(queue, name, rows):
            raw = held.tile([P, PACK, Q], F32, name=name)
            queue.dma_start(out=raw[:], in_=rows.rearrange("(p j) c -> p j c", j=PACK))
            return raw

        def load_words(name, words):
            pool_words = held.tile([P, T], U32, name=name)
            nc.sync.dma_start(out=pool_words[:].bitcast(I32), in_=words[0].rearrange("p n j -> p (n j)").bitcast(I32))
            return pool_words

        def load_scales(plane, scales):
            for r in range(4):
                nc.sync.dma_start(out=plane[r:P:32, :].bitcast(I32), in_=scales[0][r:16:4, :].bitcast(I32))

        def quantise(name, grouped, tag=None):
            codes = held.tile([P, Q], U32, name=name + "_codes", tag=tag or name + "_codes", align_bytes=64)
            plane = held.tile([P, Q], U8, name=name + "_plane", align_bytes=64)
            nc.vector.quantize_mx(out=codes[:].bitcast(FP8X4), scales=plane[:], in_=grouped[:].rearrange("p c j -> p (c j)"))
            return codes, plane

        def product(acc, rows, words, plane):
            nc.tensor.matmul_mx(out=acc, lhsT=rows[0][:].bitcast(FP8X4), lhsT_scale=rows[1][:], rhs=words.bitcast(FP8X4), rhs_scale=plane, start=True, stop=True)

        key_plane = held.tile([P, T], U8, name="key_plane")
        val_plane = held.tile([P, T], U8, name="val_plane")
        nc.vector.memset(key_plane[:, : T // 2].bitcast(I32), 0)
        nc.gpsimd.memset(key_plane[:, T // 2 :].bitcast(I32), 0)
        nc.vector.memset(val_plane[: P - 16, :].bitcast(I32), 0)
        val_plane_mx = held.tile([P, SLOTS], U8, name="val_plane_mx", align_bytes=64)
        nc.gpsimd.memset(val_plane_mx[:].bitcast(I32), 0)

        query2_raw = load_rows(nc.sync, "query2_raw", query2)
        offsets = held.tile([P, SLOTS // LIST_ROWS], U16, name="offsets")
        nc.sync.dma_start(offsets[:], offs)
        nc.sync.dma_start(out=val_plane[P - 16 :, :].bitcast(I32), in_=vals_scales[0].bitcast(I32))
        load_scales(key_plane, keys_scales)
        key_words = load_words("key_words", keys_words)
        query_raw = load_rows(nc.sync, "query_raw", query)
        val_words = load_words("val_words", vals_words)
        gout_raw = load_rows(nc.sync, "gout_raw", gout)
        strictness = column("strictness")
        nc.sync.dma_start(out=strictness[:], in_=strict)
        base_sb = wide("base_sb")
        nc.sync.dma_start(out=base_sb[:], in_=base)

        query2_bf = held.tile([P, Q, PACK], BF16, name="query2_bf", align_bytes=64)
        nc.scalar.activation(out=query2_bf[:], in_=query2_raw[:].rearrange("p j c -> p c j"), func=ACT.Copy)

        val_plane_g = held.tile([P, SLOTS], U8, name="val_plane_g", align_bytes=64)
        nc.vector.tensor_copy(val_plane_g[:], val_plane[:].indirect(offsets[:]))
        key_plane_g = held.tile([P, SLOTS], U8, name="key_plane_g", align_bytes=64)
        nc.vector.tensor_copy(key_plane_g[:], key_plane[:].indirect(offsets[:]))
        for r in range(4):
            nc.sync.dma_start(out=val_plane_mx[r:P:32, :].bitcast(I32), in_=val_plane_g[P - 16 + r : P : 4, :].bitcast(I32))
        query2_mx = quantise("query2", query2_bf)
        key_words_g = held.tile([P, SLOTS], U32, name="key_words_g", align_bytes=64)
        b_half = [psum.tile([P, HALF], F32, name="b_half%d" % h) for h in range(2)]
        exp_b = wide("exp_b", tag="query_raw")
        cols = HALF // LIST_ROWS
        for h in range(2):
            nc.vector.tensor_copy(key_words_g[:, halves[h]], key_words[:].indirect(offsets[:, h * cols : (h + 1) * cols]))
            product(b_half[h][:], query2_mx, key_words_g[:, halves[h]], key_plane_g[:, halves[h]])

        query_bf = held.tile([P, Q, PACK], BF16, name="query_bf", align_bytes=64)
        nc.scalar.activation(out=query_bf[:], in_=query_raw[:].rearrange("p j c -> p c j"), func=ACT.Copy)
        for h in range(2):
            nc.scalar.activation(out=exp_b[:, halves[h]], in_=b_half[h][:], func=ACT.Exp)
        query_mx = quantise("query", query_bf)
        a_acc = psum.tile([P, SLOTS], F32, name="a_acc")
        product(a_acc[:], query_mx, key_words_g[:], key_plane_g[:])

        exp_capped = wide("exp_capped")
        log_part = held.tile([P, SLOTS], F32, name="log_part", align_bytes=64)
        for h in range(2):
            nc.vector.tensor_scalar(exp_capped[:, halves[h]], exp_b[:, halves[h]], math.exp(CAP), 0.0, ALU.min, ALU.max)
        for h in range(2):
            nc.scalar.activation(out=log_part[:, halves[h]], in_=exp_capped[:, halves[h]], func=ACT.Ln, bias=1.0)

        first, second = halves
        b_first = column("b_first", HALF)
        nc.vector.tensor_copy(b_first[:], b_half[0][:])
        a_plus_b = column("a_plus_b", HALF)
        nc.vector.tensor_tensor(a_plus_b[:], a_acc[:, first], b_first[:], ALU.add)
        val_words_g = held.tile([P, SLOTS], U32, name="val_words_g", align_bytes=64)
        nc.vector.tensor_copy(val_words_g[:], val_words[:].indirect(offsets[:]))

        gout_bf = held.tile([P, Q, PACK], BF16, name="gout_bf", align_bytes=64)
        nc.gpsimd.tensor_scalar(gout_bf[:], gout_raw[:].rearrange("p j c -> p c j"), 1.0, 0.0, ALU.mult, ALU.add)

        line = column("line", 2)
        one_plus = line[:, 0:1]
        strict_pair = column("strict_pair", 2)
        nc.gpsimd.tensor_scalar(one_plus, strictness[:], 1.0, 1.0, ALU.mult, ALU.add)
        nc.gpsimd.tensor_scalar(line[:, 1:2], strictness[:], -1.0, 0.0, ALU.mult, ALU.add)
        nc.gpsimd.tensor_scalar(strict_pair[:, 0:1], strictness[:], 1.0, 0.0, ALU.mult, ALU.add)
        nc.gpsimd.tensor_scalar(strict_pair[:, 1:2], strictness[:], ROOT_K, 0.0, ALU.mult, ALU.add)

        soft = wide("soft", tag="val_words")
        for h in range(2):
            nc.vector.tensor_tensor(soft[:, halves[h]], b_half[h][:], log_part[:, halves[h]], ALU.max)
        neg_s = wide("neg_s")
        for h in range(2):
            nc.vector.scalar_tensor_tensor(neg_s[:, halves[h]], soft[:, halves[h]], strictness[:], a_acc[:, halves[h]], ALU.mult, ALU.subtract)
        gout_mx = quantise("gout", gout_bf, tag="log_part")
        c_acc = psum.tile([P, SLOTS], F32, name="c_acc")
        product(c_acc[:], gout_mx, val_words_g[:], val_plane_mx[:])
        neg_max = column("neg_max")
        nc.vector.tensor_reduce(neg_max[:], neg_s[:], AXIS_X, ALU.min)
        p = wide("p")
        z = column("z")
        nc.scalar.activation(out=p[:], in_=neg_s[:], func=ACT.Exp, bias=neg_max[:], scale=-1.0, accum_out=z[:])
        neg_s2 = held.tile([P, SLOTS], F32, name="neg_s2", tag="gout_bf", align_bytes=64)
        without_b = column("without_b", HALF)
        nc.vector.scalar_tensor_tensor(without_b[:], soft[:, second], one_plus, a_acc[:, second], ALU.mult, ALU.subtract)
        nc.vector.scalar_tensor_tensor(neg_s2[:, first], soft[:, first], one_plus, a_plus_b[:], ALU.mult, ALU.subtract)
        nc.vector.tensor_tensor(neg_s2[:, second], without_b[:], b_half[1][:], ALU.subtract)
        t = wide("t")
        nc.scalar.activation(out=t[:], in_=neg_s2[:], func=ACT.Exp, bias=neg_max[:], scale=-1.0)
        rest = held.tile([P, SLOTS], F32, name="rest", tag="gout_bf", align_bytes=64)
        nc.scalar.activation(out=rest[:], in_=soft[:], func=ACT.Exp, scale=-1.0)
        inv_z = column("inv_z")
        nc.vector.reciprocal(inv_z[:], z[:])
        c_mean = column("c_mean")
        weighted = wide("weighted")
        nc.vector.scalar_tensor_tensor(weighted[:], c_acc[:], inv_z[:], p[:], ALU.mult, ALU.mult, accum_out=c_mean[:])
        kappa = column("kappa", 2)
        nc.gpsimd.tensor_scalar(kappa[:], strict_pair[:], inv_z[:], 0.0, ALU.mult, ALU.add)
        scaled_line = column("scaled_line", 2)
        nc.gpsimd.tensor_scalar(scaled_line[:], line[:], kappa[:, 1:2], kappa[:, 1:2], ALU.mult, ALU.mult)
        curve = wide("curve")
        nc.scalar.activation(out=curve[:], in_=rest[:], func=ACT.Identity, bias=scaled_line[:, 1:2], scale=scaled_line[:, 0:1])
        v = wide("v")
        nc.vector.scalar_tensor_tensor(v[:], c_acc[:], c_mean[:], t[:], ALU.subtract, ALU.mult)
        cubed = column("cubed")
        nc.gpsimd.tensor_scalar(cubed[:], kappa[:, 1:2], kappa[:, 1:2], kappa[:, 0:1], ALU.mult, ALU.mult)

        squares = wide("squares")
        m_sum = column("m_sum")
        nc.scalar.activation(out=squares[:], in_=v[:], func=ACT.Square, scale=kappa[:, 1:2], accum_out=m_sum[:])
        m_coef = column("m_coef")
        nc.scalar.activation(out=m_coef[:], in_=m_sum[:], func=ACT.Copy, scale=kappa[:, 0:1])

        h_terms = wide("h_terms")
        h_coef = column("h_coef")
        nc.vector.scalar_tensor_tensor(h_terms[:], v[:], cubed[:], t[:], ALU.mult, ALU.mult, accum_out=h_coef[:])
        curved = wide("curved")
        with_h = wide("with_h")
        with_m = wide("with_m")
        result = wide("result")
        for part in halves:
            nc.vector.tensor_tensor(curved[:, part], curve[:, part], v[:, part], ALU.mult)
        for part in halves:
            nc.vector.scalar_tensor_tensor(with_h[:, part], curved[:, part], h_coef[:], v[:, part], ALU.add, ALU.mult)
        for part in halves:
            nc.vector.scalar_tensor_tensor(with_m[:, part], t[:, part], m_coef[:], base_sb[:, part], ALU.mult, ALU.add)
        for part in halves:
            nc.vector.tensor_tensor(result[:, part], with_m[:, part], with_h[:, part], ALU.add)
            nc.sync.dma_start(out=out[:, part], in_=result[:, part])
